import numpy as np
import ml_dtypes


def mxq(x, axis, fmt="e4m3"):
    dtype, down = {"e4m3": (ml_dtypes.float8_e4m3fn, 7), "e5m2": (ml_dtypes.float8_e5m2, 14)}[fmt]
    v = np.moveaxis(np.asarray(x, np.float32).astype(ml_dtypes.bfloat16).astype(np.float64), axis, -1)
    blocks = v.reshape(v.shape[:-1] + (-1, 32))
    amax = np.abs(blocks).max(-1, keepdims=True)
    byte = np.maximum(np.where(amax > 0, np.frexp(amax)[1] - 1 + 127, 0) - down, 1)
    scale = np.exp2(byte - 127.0)
    codes = (blocks / scale).astype(np.float32).astype(dtype).astype(np.float64)
    return np.moveaxis((codes * scale).reshape(v.shape), -1, axis)


WIDE = False


def mx_kscale(k):
    if not WIDE:
        return np.ones(k)
    levels = np.array([10, -10, 5, -5, 0])
    if k % 512:
        return np.exp2(np.random.permutation(np.resize(levels, k // 32))).repeat(32)
    a = np.empty((k // 512, 16))
    for p in range(k // 512):
        a[p, :8] = np.random.permutation(np.resize(levels, 8))
        for g in range(8):
            far = levels[np.abs(levels - a[p, g]) >= 10]
            a[p, g + 8] = far[np.random.randint(len(far))]
    return np.exp2(a.ravel()).repeat(32)


def f64(x):
    return np.asarray(x).astype(np.float64)


def striped8(idx):
    return np.asarray(idx).reshape(8, -1, 16).transpose(0, 2, 1).reshape(128, -1).astype(np.uint16)


def unstriped8(offs):
    return offs.reshape(8, 16, -1).transpose(0, 2, 1).reshape(8, -1).astype(np.int64)


def pick8(x, idx, run):
    r = np.arange(len(x))
    return x[r[:, None], idx[r % (8 * run) // run]]


E2M1 = np.array([0.0, 0.5, 1.0, 1.5, 2.0, 3.0, 4.0, 6.0, -0.0, -0.5, -1.0, -1.5, -2.0, -3.0, -4.0, -6.0])


def pack_weight(w, fmt):
    k, n = w.shape
    w = f64(np.asarray(w, np.float32).astype(ml_dtypes.bfloat16)).reshape(k // 32, 32, n)
    amax = np.abs(w).max(1)
    if fmt == "e4m3":
        byte = np.frexp(amax)[1] - 1 + 127 - 7
    else:
        mant, ex = np.frexp(amax / 6.0)
        byte = np.where(mant > 0.5, ex, ex - 1) + 127
    byte = np.clip(np.where(amax > 0, byte, 1), 1, 254)
    scaled = (w * np.exp2(127.0 - byte)[:, None, :]).reshape(k, n).astype(np.float32)
    by_word = np.ascontiguousarray(scaled.reshape(k // 512, 128, 4, n).transpose(0, 1, 3, 2))
    if fmt == "e4m3":
        words = by_word.astype(ml_dtypes.float8_e4m3fn).view(np.uint8)
    else:
        c = by_word.astype(ml_dtypes.float4_e2m1fn).view(np.uint8) & 0xF
        words = (c[..., 0::2] | (c[..., 1::2] << 4)).reshape(k // 512, 128, 2 * n)
    return np.ascontiguousarray(words), np.ascontiguousarray(byte.astype(np.uint8).reshape(k // 512, 16, n))


def unpack_weight(words, scales, fmt):
    g, _, n = scales.shape
    words = np.ascontiguousarray(words).reshape(g, 128, n, -1)
    if fmt == "e4m3":
        vals = words.view(ml_dtypes.float8_e4m3fn).astype(np.float64)
    else:
        nib = np.empty((g, 128, n, 4), np.uint8)
        nib[..., 0::2] = words & 0xF
        nib[..., 1::2] = words >> 4
        vals = E2M1[nib]
    vals = vals * np.repeat(np.exp2(scales.astype(np.float64) - 127.0), 8, axis=1)[..., None]
    return vals.transpose(0, 1, 3, 2).reshape(g * 512, n)


def sigmoid(v):
    return 1.0 / (1.0 + np.exp(-v))


D, V, Q, I = 512, 2048, 128, 512


def setup_inputs():
    n = np.random.standard_normal
    idx = np.stack([np.random.permutation(V)[:I] for _ in range(8)])
    idx2 = np.stack([np.random.permutation(V)[:I] for _ in range(8)])
    fd = mx_kscale(D)
    vocp = pack_weight(n((D, V)) / fd[:, None], "e2m1")
    return {
        "hid": (n((D, Q)) * 1.0 / np.sqrt(D) * fd[:, None]).astype(np.float32),
        "voc_words": vocp[0],
        "voc_scales": vocp[1],
        "sw": (np.random.uniform(0.5, 2.0, (1, I))).astype(np.float32),
        "old": (0.5 * n((Q, V))).astype(np.float32),
        "offs": striped8(idx),
        "offs2": striped8(idx2),
    }


def reference(hid, voc_words, voc_scales, sw, old, offs, offs2):
    idx = unstriped8(offs)
    idx2 = unstriped8(offs2)
    vocu = unpack_weight(voc_words, voc_scales, "e2m1")
    hidq = mxq(f64(hid), 0, "e4m3")
    a = hidq.T @ vocu
    m1 = np.max(a, axis=1, keepdims=True)
    p = np.exp(a - m1)
    z = np.sum(p, axis=1, keepdims=True)
    px = np.exp(pick8(a, idx, 16) - m1)
    px2 = np.exp(pick8(a, idx2, 16) - m1)
    u1 = sigmoid((px2 - px) / z * 512.0)
    dpx2 = f64(sw) * u1 * (1.0 - u1) * 512.0 / z
    dpx = f64(sw) * u1 * (1.0 - u1) * 512.0 / z * (-1.0)
    dz = np.sum(f64(sw) * u1 * (1.0 - u1) * 512.0 * (px2 - px) / np.square(z) * (-1.0), axis=1, keepdims=True)
    e1 = dpx2 * px2
    s1 = np.zeros((Q, V))
    s1[np.arange(Q)[:, None], idx2[np.arange(Q) % 128 // 16]] = e1
    e2 = dpx * px
    s2 = np.zeros((Q, V))
    s2[np.arange(Q)[:, None], idx[np.arange(Q) % 128 // 16]] = e2
    da = dz * p + s1 + s2
    y = da * 2.0 + f64(old)
    return y

@@ -1,0 +1,216 @@
+from contextlib import ExitStack
+
+import concourse.mybir as mybir
+from concourse.masks import make_identity
+
+D, V, Q, I = 512, 2048, 128, 512
+FLOPS = 2 * D * Q * V
+
+F32 = mybir.dt.float32
+BF16 = mybir.dt.bfloat16
+I32 = mybir.dt.int32
+U32 = mybir.dt.uint32
+U16 = mybir.dt.uint16
+U8 = mybir.dt.uint8
+FP8X4 = mybir.dt.float8_e4m3fn_x4
+FP4X4 = mybir.dt.float4_e2m1fn_x4
+ALU = mybir.AluOpType
+ACT = mybir.ActivationFunctionType
+AXIS = mybir.AxisListType
+
+P = 128
+PACK = 4
+BANK = 512
+BANKS = V // BANK
+BLOCKS = BANK // P
+WORD_LOADS = 2
+PIECE_EDGES = (0, 128, I)
+PIECES = len(PIECE_EDGES) - 1
+PER_COLUMN = 16
+
+
+def tile_attend_brankshares_heads_kernel(tc, hid, voc_words, voc_scales, sw, old, offs, offs2, out):
+    nc = tc.nc
+    with ExitStack() as ctx:
+        sb = ctx.enter_context(tc.tile_pool(name="sb", bufs=1))
+        ps = ctx.enter_context(tc.psum_pool(name="ps", bufs=1))
+
+        hid_raw = sb.tile([P, PACK, Q], F32, name="hid_raw")
+        nc.sync.dma_start(out=hid_raw[:], in_=hid.rearrange("(p t) q -> p t q", t=PACK))
+
+        voc_plane = sb.tile([P, V], U8, name="voc_plane", align_bytes=64)
+        nc.gpsimd.memset(voc_plane[:].bitcast(I32), 0)
+        for quad in range(4):
+            nc.sync.dma_start(
+                out=voc_plane[32 * quad : 32 * quad + 4, :].bitcast(I32),
+                in_=voc_scales[0, 4 * quad : 4 * quad + 4, :].bitcast(I32),
+            )
+        load_bytes = 2 * V // WORD_LOADS
+        words = []
+        for w in range(WORD_LOADS):
+            part = sb.tile([P, load_bytes], U8, name="words%d" % w, align_bytes=64)
+            nc.sync.dma_start(
+                out=part[:].bitcast(I32),
+                in_=voc_words[0, :, w * load_bytes : (w + 1) * load_bytes].bitcast(I32),
+            )
+            words.append(part)
+        list1 = sb.tile([P, I // PER_COLUMN], U16, name="list1")
+        nc.sync.dma_start(list1[:], offs)
+        list2 = sb.tile([P, I // PER_COLUMN], U16, name="list2")
+        nc.sync.dma_start(list2[:], offs2)
+        weight = sb.tile([P, I], F32, name="weight")
+        nc.sync.dma_start(out=weight[:], in_=sw[0].partition_broadcast(P))
+        old_sb = sb.tile([P, V], F32, name="old_sb")
+        nc.sync.dma_start(out=old_sb[:], in_=old)
+
+        ident = sb.tile([P, P], F32, name="ident")
+        make_identity(nc, ident[:])
+        placed1 = sb.tile([P, V], F32, name="placed1")
+        nc.vector.memset(placed1[:], 0.0)
+
+        hid_bf = sb.tile([P, Q, PACK], BF16, name="hid_bf", tag="hid_then_placed", align_bytes=64)
+        hid_codes = sb.tile([P, Q], U32, name="hid_codes", align_bytes=64)
+        hid_plane = sb.tile([P, Q], U8, name="hid_plane", align_bytes=64)
+        row_halves = [slice(0, Q // 2), slice(Q // 2, Q)]
+        for rows in row_halves:
+            nc.vector.tensor_copy(out=hid_bf[:, rows, :], in_=hid_raw[:, :, rows].rearrange("p t q -> p q t"))
+        for rows in row_halves:
+            nc.vector.quantize_mx(
+                out=hid_codes[:, rows].bitcast(FP8X4), scales=hid_plane[:, rows],
+                in_=hid_bf[:, rows, :].rearrange("p q t -> p (q t)"),
+            )
+        placed2 = sb.tile([P, V], F32, name="placed2", tag="hid_then_placed", align_bytes=64)
+        nc.gpsimd.memset(placed2[:], 0.0)
+
+        scores = sb.tile([P, V], F32, name="scores")
+        bank_max = sb.tile([P, BANKS], F32, name="bank_max")
+        shares = sb.tile([P, V], F32, name="shares")
+
+        def columns(b):
+            return slice(b * BANK, (b + 1) * BANK)
+
+        def score(b):
+            acc = ps.tile([P, BANK], F32, name="upright%d" % b, tag="upright%d" % b)
+            per_load = BANKS // WORD_LOADS
+            first = (b % per_load) * 2 * BANK
+            nc.tensor.matmul_mx(
+                out=acc[:],
+                lhsT=hid_codes[:].bitcast(FP8X4),
+                lhsT_scale=hid_plane[:],
+                rhs=words[b // per_load][:, first : first + 2 * BANK].bitcast(FP4X4),
+                rhs_scale=voc_plane[:, columns(b)],
+                start=True,
+                stop=True,
+            )
+            nc.vector.tensor_scalar(
+                out=scores[:, columns(b)], in0=acc[:], scalar1=1.0, scalar2=None,
+                op0=ALU.mult, op1=ALU.max, accum_out=bank_max[:, b : b + 1],
+            )
+
+        for b in range(BANKS):
+            score(b)
+        neg_m1 = sb.tile([P, 1], F32, name="neg_m1")
+        nc.vector.tensor_reduce(out=neg_m1[:], in_=bank_max[:], axis=AXIS.X, op=ALU.max, negate=True)
+        z = sb.tile([P, 1], F32, name="z")
+        nc.scalar.activation(out=shares[:], in_=scores[:], func=ACT.Exp, bias=neg_m1[:], accum_out=z[:])
+
+        picked = sb.tile([P, 2, I], F32, name="picked")
+        nc.vector.tensor_copy(out=picked[:, 0, :], in_=scores[:].indirect(list1[:]))
+        nc.vector.tensor_copy(out=picked[:, 1, :], in_=scores[:].indirect(list2[:]))
+
+        inv_z = sb.tile([P, 1], F32, name="inv_z")
+        nc.vector.reciprocal(out=inv_z[:], in_=z[:])
+        rate = sb.tile([P, 1], F32, name="rate")
+        nc.vector.tensor_scalar(out=rate[:], in0=inv_z[:], scalar1=256.0, scalar2=None, op0=ALU.mult)
+        weight_rate = sb.tile([P, I], F32, name="weight_rate")
+        nc.vector.tensor_scalar(
+            out=weight_rate[:], in0=weight[:], scalar1=inv_z[:], scalar2=256.0, op0=ALU.mult, op1=ALU.mult
+        )
+
+        both = sb.tile([P, 2, I], F32, name="both")
+        px = both[:, 0, :]
+        px2 = both[:, 1, :]
+        gap = sb.tile([P, I], F32, name="gap")
+        half = sb.tile([P, I], F32, name="half")
+        half_sq = sb.tile([P, I], F32, name="half_sq")
+        slope = sb.tile([P, I], F32, name="slope")
+
+        def slots(h):
+            return slice(PIECE_EDGES[h], PIECE_EDGES[h + 1])
+
+        def entries(h):
+            return slice(PIECE_EDGES[h] // PER_COLUMN, PIECE_EDGES[h + 1] // PER_COLUMN)
+
+        for h in range(PIECES):
+            nc.scalar.activation(out=both[:, :, slots(h)], in_=picked[:, :, slots(h)], func=ACT.Exp, bias=neg_m1[:])
+        for h in range(PIECES):
+            nc.vector.tensor_tensor(out=gap[:, slots(h)], in0=px2[:, slots(h)], in1=px[:, slots(h)], op=ALU.subtract)
+            nc.scalar.activation(out=half[:, slots(h)], in_=gap[:, slots(h)], func=ACT.Tanh, scale=rate[:])
+            nc.scalar.activation(out=half_sq[:, slots(h)], in_=half[:, slots(h)], func=ACT.Square)
+
+        def slope_piece(h):
+            nc.vector.scalar_tensor_tensor(
+                out=slope[:, slots(h)], in0=half_sq[:, slots(h)], scalar=1.0, in1=weight_rate[:, slots(h)],
+                op0=ALU.subtract, op1=ALU.mult,
+            )
+
+        def place1(h):
+            nc.vector.tensor_tensor(
+                out=placed1[:].indirect(list1[:, entries(h)]), in0=slope[:, slots(h)], in1=px[:, slots(h)], op=ALU.mult
+            )
+
+        slope_piece(0)
+        place1(0)
+        slope_piece(1)
+        slope_gap = sb.tile([P, I], F32, name="slope_gap")
+        total = sb.tile([P, 1], F32, name="total")
+        nc.vector.scalar_tensor_tensor(
+            out=slope_gap[:], in0=slope[:], scalar=inv_z[:], in1=gap[:], op0=ALU.mult, op1=ALU.mult, accum_out=total[:]
+        )
+        place1(1)
+        nc.vector.tensor_tensor(out=placed2[:].indirect(list2[:]), in0=slope[:], in1=px2, op=ALU.mult)
+
+        spread = sb.tile([P, V], F32, name="spread")
+        for b in range(BANKS):
+            nc.scalar.activation(
+                out=spread[:, columns(b)], in_=shares[:, columns(b)], func=ACT.Copy, scale=total[:]
+            )
+
+        turned = [ps.tile([P, BANK], F32, name="turned%d" % b, tag="turned%d" % b) for b in range(BANKS)]
+        addends = [old_sb, spread, placed1]
+
+        def add_turned(b, n):
+            for j in range(BLOCKS):
+                first = b * BANK + j * P
+                nc.tensor.matmul(
+                    turned[b][:, j * P : (j + 1) * P], addends[n][:, first : first + P], ident[:],
+                    start=(n == 0 and j == 0), stop=(n == len(addends) - 1 and j == BLOCKS - 1),
+                    is_transpose=True,
+                )
+
+        for n in range(len(addends) - 1):
+            for b in range(BANKS):
+                add_turned(b, n)
+
+        turned_sb = sb.tile([P, V], F32, name="turned_sb")
+        result = sb.tile([P, V], F32, name="result")
+
+        def close_sum(b):
+            add_turned(b, len(addends) - 1)
+            nc.scalar.copy(out=turned_sb[:, columns(b)], in_=turned[b][:])
+
+        def finish(b):
+            back = ps.tile([P, BANK], F32, name="back%d" % b, tag="upright%d" % b)
+            for j in range(BLOCKS):
+                first = b * BANK + j * P
+                nc.tensor.transpose(back[:, j * P : (j + 1) * P], turned_sb[:, first : first + P], ident[:])
+            nc.vector.tensor_tensor(
+                out=result[:, columns(b)], in0=back[:], in1=placed2[:, columns(b)], op=ALU.subtract
+            )
+            nc.sync.dma_start(out=out[:, columns(b)], in_=result[:, columns(b)])
+
+        for b in range(BANKS + 2):
+            if b < BANKS:
+                close_sum(b)
+            if b > 1:
+                finish(b - 2)

@@ -23,7 +23,7 @@ PACK = 4
 BANK = 512
 BANKS = V // BANK
 BLOCKS = BANK // P
-WORD_LOADS = 2
+LOAD_EDGES = (0, BANK, 2 * BANK, V)
 PIECE_EDGES = (0, 128, I)
 PIECES = len(PIECE_EDGES) - 1
 PER_COLUMN = 16
@@ -45,15 +45,12 @@ def tile_attend_brankshares_heads_kernel(tc, hid, voc_words, voc_scales, sw, old
                 out=voc_plane[32 * quad : 32 * quad + 4, :].bitcast(I32),
                 in_=voc_scales[0, 4 * quad : 4 * quad + 4, :].bitcast(I32),
             )
-        load_bytes = 2 * V // WORD_LOADS
         words = []
-        for w in range(WORD_LOADS):
-            part = sb.tile([P, load_bytes], U8, name="words%d" % w, align_bytes=64)
-            nc.sync.dma_start(
-                out=part[:].bitcast(I32),
-                in_=voc_words[0, :, w * load_bytes : (w + 1) * load_bytes].bitcast(I32),
-            )
-            words.append(part)
+        for first, last in zip(LOAD_EDGES, LOAD_EDGES[1:]):
+            part = sb.tile([P, 2 * (last - first)], U8, name="words%d" % first, align_bytes=64)
+            nc.sync.dma_start(out=part[:].bitcast(I32), in_=voc_words[0, :, 2 * first : 2 * last].bitcast(I32))
+            for start in range(0, last - first, BANK):
+                words.append(part[:, 2 * start : 2 * (start + BANK)])
         list1 = sb.tile([P, I // PER_COLUMN], U16, name="list1")
         nc.sync.dma_start(list1[:], offs)
         list2 = sb.tile([P, I // PER_COLUMN], U16, name="list2")
@@ -71,14 +68,13 @@ def tile_attend_brankshares_heads_kernel(tc, hid, voc_words, voc_scales, sw, old
         hid_bf = sb.tile([P, Q, PACK], BF16, name="hid_bf", tag="hid_then_placed", align_bytes=64)
         hid_codes = sb.tile([P, Q], U32, name="hid_codes", align_bytes=64)
         hid_plane = sb.tile([P, Q], U8, name="hid_plane", align_bytes=64)
-        row_halves = [slice(0, Q // 2), slice(Q // 2, Q)]
-        for rows in row_halves:
-            nc.vector.tensor_copy(out=hid_bf[:, rows, :], in_=hid_raw[:, :, rows].rearrange("p t q -> p q t"))
-        for rows in row_halves:
-            nc.vector.quantize_mx(
-                out=hid_codes[:, rows].bitcast(FP8X4), scales=hid_plane[:, rows],
-                in_=hid_bf[:, rows, :].rearrange("p q t -> p (q t)"),
-            )
+        nc.vector.tensor_copy(
+            out=hid_bf[:, : Q // 2, :], in_=hid_raw[:, :, : Q // 2].rearrange("p t q -> p q t")
+        )
+        nc.scalar.copy(out=hid_bf[:, Q // 2 :, :], in_=hid_raw[:, :, Q // 2 :].rearrange("p t q -> p q t"))
+        nc.vector.quantize_mx(
+            out=hid_codes[:].bitcast(FP8X4), scales=hid_plane[:], in_=hid_bf[:].rearrange("p q t -> p (q t)")
+        )
         placed2 = sb.tile([P, V], F32, name="placed2", tag="hid_then_placed", align_bytes=64)
         nc.gpsimd.memset(placed2[:], 0.0)
 
@@ -91,13 +87,11 @@ def tile_attend_brankshares_heads_kernel(tc, hid, voc_words, voc_scales, sw, old
 
         def score(b):
             acc = ps.tile([P, BANK], F32, name="upright%d" % b, tag="upright%d" % b)
-            per_load = BANKS // WORD_LOADS
-            first = (b % per_load) * 2 * BANK
             nc.tensor.matmul_mx(
                 out=acc[:],
                 lhsT=hid_codes[:].bitcast(FP8X4),
                 lhsT_scale=hid_plane[:],
-                rhs=words[b // per_load][:, first : first + 2 * BANK].bitcast(FP4X4),
+                rhs=words[b].bitcast(FP4X4),
                 rhs_scale=voc_plane[:, columns(b)],
                 start=True,
                 stop=True,
@@ -107,17 +101,37 @@ def tile_attend_brankshares_heads_kernel(tc, hid, voc_words, voc_scales, sw, old
                 op0=ALU.mult, op1=ALU.max, accum_out=bank_max[:, b : b + 1],
             )
 
-        for b in range(BANKS):
-            score(b)
-        neg_m1 = sb.tile([P, 1], F32, name="neg_m1")
-        nc.vector.tensor_reduce(out=neg_m1[:], in_=bank_max[:], axis=AXIS.X, op=ALU.max, negate=True)
+        neg_max = sb.tile([P, BANKS], F32, name="neg_max")
+        bank_sum = sb.tile([P, BANKS], F32, name="bank_sum")
+
+        def exponentiate(b):
+            nc.vector.tensor_reduce(
+                out=neg_max[:, b : b + 1], in_=bank_max[:, 0 : b + 1], axis=AXIS.X, op=ALU.max, negate=True
+            )
+            nc.scalar.activation(
+                out=shares[:, columns(b)], in_=scores[:, columns(b)], func=ACT.Exp,
+                bias=neg_max[:, b : b + 1], accum_out=bank_sum[:, b : b + 1],
+            )
+
+        for b in range(BANKS + 1):
+            if b < BANKS:
+                score(b)
+            if b > 0:
+                exponentiate(b - 1)
+        neg_m1 = neg_max[:, BANKS - 1 : BANKS]
+        fix = sb.tile([P, BANKS], F32, name="fix")
+        nc.scalar.activation(out=fix[:], in_=neg_max[:], func=ACT.Exp, scale=-1.0, bias=neg_m1)
+
+        picked = sb.tile([P, I], F32, name="picked")
+        nc.vector.tensor_copy(out=picked[:], in_=scores[:].indirect(list1[:]))
+        px2 = sb.tile([P, I], F32, name="px2")
+        nc.scalar.activation(out=px2[:], in_=scores[:].indirect(list2[:]), func=ACT.Exp, bias=neg_m1)
+
+        terms = sb.tile([P, BANKS], F32, name="terms")
         z = sb.tile([P, 1], F32, name="z")
-        nc.scalar.activation(out=shares[:], in_=scores[:], func=ACT.Exp, bias=neg_m1[:], accum_out=z[:])
-
-        picked = sb.tile([P, 2, I], F32, name="picked")
-        nc.vector.tensor_copy(out=picked[:, 0, :], in_=scores[:].indirect(list1[:]))
-        nc.vector.tensor_copy(out=picked[:, 1, :], in_=scores[:].indirect(list2[:]))
-
+        nc.vector.scalar_tensor_tensor(
+            out=terms[:], in0=fix[:], scalar=1.0, in1=bank_sum[:], op0=ALU.mult, op1=ALU.mult, accum_out=z[:]
+        )
         inv_z = sb.tile([P, 1], F32, name="inv_z")
         nc.vector.reciprocal(out=inv_z[:], in_=z[:])
         rate = sb.tile([P, 1], F32, name="rate")
@@ -127,9 +141,7 @@ def tile_attend_brankshares_heads_kernel(tc, hid, voc_words, voc_scales, sw, old
             out=weight_rate[:], in0=weight[:], scalar1=inv_z[:], scalar2=256.0, op0=ALU.mult, op1=ALU.mult
         )
 
-        both = sb.tile([P, 2, I], F32, name="both")
-        px = both[:, 0, :]
-        px2 = both[:, 1, :]
+        px = sb.tile([P, I], F32, name="px")
         gap = sb.tile([P, I], F32, name="gap")
         half = sb.tile([P, I], F32, name="half")
         half_sq = sb.tile([P, I], F32, name="half_sq")
@@ -142,7 +154,7 @@ def tile_attend_brankshares_heads_kernel(tc, hid, voc_words, voc_scales, sw, old
             return slice(PIECE_EDGES[h] // PER_COLUMN, PIECE_EDGES[h + 1] // PER_COLUMN)
 
         for h in range(PIECES):
-            nc.scalar.activation(out=both[:, :, slots(h)], in_=picked[:, :, slots(h)], func=ACT.Exp, bias=neg_m1[:])
+            nc.scalar.activation(out=px[:, slots(h)], in_=picked[:, slots(h)], func=ACT.Exp, bias=neg_m1)
         for h in range(PIECES):
             nc.vector.tensor_tensor(out=gap[:, slots(h)], in0=px2[:, slots(h)], in1=px[:, slots(h)], op=ALU.subtract)
             nc.scalar.activation(out=half[:, slots(h)], in_=gap[:, slots(h)], func=ACT.Tanh, scale=rate[:])
@@ -160,20 +172,29 @@ def tile_attend_brankshares_heads_kernel(tc, hid, voc_words, voc_scales, sw, old
             )
 
         slope_piece(0)
+        weighted_gap = sb.tile([P, I], F32, name="weighted_gap")
+        nc.vector.scalar_tensor_tensor(
+            out=weighted_gap[:], in0=gap[:], scalar=inv_z[:], in1=weight_rate[:], op0=ALU.mult, op1=ALU.mult
+        )
         place1(0)
-        slope_piece(1)
         slope_gap = sb.tile([P, I], F32, name="slope_gap")
         total = sb.tile([P, 1], F32, name="total")
         nc.vector.scalar_tensor_tensor(
-            out=slope_gap[:], in0=slope[:], scalar=inv_z[:], in1=gap[:], op0=ALU.mult, op1=ALU.mult, accum_out=total[:]
+            out=slope_gap[:], in0=half_sq[:], scalar=1.0, in1=weighted_gap[:], op0=ALU.subtract, op1=ALU.mult,
+            accum_out=total[:],
         )
+        slope_piece(1)
         place1(1)
-        nc.vector.tensor_tensor(out=placed2[:].indirect(list2[:]), in0=slope[:], in1=px2, op=ALU.mult)
+        nc.vector.tensor_tensor(out=placed2[:].indirect(list2[:]), in0=slope[:], in1=px2[:], op=ALU.mult)
 
+        factor = sb.tile([P, BANKS - 1], F32, name="factor")
+        nc.scalar.activation(out=factor[:], in_=fix[:, 0 : BANKS - 1], func=ACT.Copy, scale=total[:])
         spread = sb.tile([P, V], F32, name="spread")
-        for b in range(BANKS):
+        order = [BANKS - 1] + list(range(BANKS - 1))
+        for b in order:
             nc.scalar.activation(
-                out=spread[:, columns(b)], in_=shares[:, columns(b)], func=ACT.Copy, scale=total[:]
+                out=spread[:, columns(b)], in_=shares[:, columns(b)], func=ACT.Copy,
+                scale=total[:] if b == BANKS - 1 else factor[:, b : b + 1],
             )
 
         turned = [ps.tile([P, BANK], F32, name="turned%d" % b, tag="turned%d" % b) for b in range(BANKS)]
@@ -189,7 +210,7 @@ def tile_attend_brankshares_heads_kernel(tc, hid, voc_words, voc_scales, sw, old
                 )
 
         for n in range(len(addends) - 1):
-            for b in range(BANKS):
+            for b in order:
                 add_turned(b, n)
 
         turned_sb = sb.tile([P, V], F32, name="turned_sb")
@@ -211,6 +232,6 @@ def tile_attend_brankshares_heads_kernel(tc, hid, voc_words, voc_scales, sw, old
 
         for b in range(BANKS + 2):
             if b < BANKS:
-                close_sum(b)
+                close_sum(order[b])
             if b > 1:
-                finish(b - 2)
+                finish(order[b - 2])

@@ -27,6 +27,7 @@ LOAD_EDGES = (0, BANK, 2 * BANK, V)
 PIECE_EDGES = (0, 128, I)
 PIECES = len(PIECE_EDGES) - 1
 PER_COLUMN = 16
+SPACED = 8
 
 
 def tile_attend_brankshares_heads_kernel(tc, hid, voc_words, voc_scales, sw, old, offs, offs2, out):
@@ -76,7 +77,7 @@ def tile_attend_brankshares_heads_kernel(tc, hid, voc_words, voc_scales, sw, old
             out=hid_codes[:].bitcast(FP8X4), scales=hid_plane[:], in_=hid_bf[:].rearrange("p q t -> p (q t)")
         )
         placed2 = sb.tile([P, V], F32, name="placed2", tag="hid_then_placed", align_bytes=64)
-        nc.gpsimd.memset(placed2[:], 0.0)
+        nc.vector.memset(placed2[:], 0.0)
 
         scores = sb.tile([P, V], F32, name="scores")
         bank_max = sb.tile([P, BANKS], F32, name="bank_max")
@@ -101,26 +102,30 @@ def tile_attend_brankshares_heads_kernel(tc, hid, voc_words, voc_scales, sw, old
                 op0=ALU.mult, op1=ALU.max, accum_out=bank_max[:, b : b + 1],
             )
 
-        neg_max = sb.tile([P, BANKS], F32, name="neg_max")
+        neg_max = sb.tile([P, BANKS, SPACED], F32, name="neg_max")
         bank_sum = sb.tile([P, BANKS], F32, name="bank_sum")
 
         def exponentiate(b):
-            nc.vector.tensor_reduce(
-                out=neg_max[:, b : b + 1], in_=bank_max[:, 0 : b + 1], axis=AXIS.X, op=ALU.max, negate=True
-            )
+            if b < BANKS - 1:
+                nc.gpsimd.tensor_scalar(
+                    out=neg_max[:, b, 0:1], in0=bank_max[:, b : b + 1], scalar1=-1.0, scalar2=0.0,
+                    op0=ALU.mult, op1=ALU.add,
+                )
+            else:
+                nc.vector.tensor_reduce(
+                    out=neg_max[:, b, 0:1], in_=bank_max[:], axis=AXIS.X, op=ALU.max, negate=True
+                )
             nc.scalar.activation(
                 out=shares[:, columns(b)], in_=scores[:, columns(b)], func=ACT.Exp,
-                bias=neg_max[:, b : b + 1], accum_out=bank_sum[:, b : b + 1],
+                bias=neg_max[:, b, 0:1], accum_out=bank_sum[:, b : b + 1],
             )
 
-        for b in range(BANKS + 1):
-            if b < BANKS:
-                score(b)
-            if b > 0:
-                exponentiate(b - 1)
-        neg_m1 = neg_max[:, BANKS - 1 : BANKS]
+        for b in range(BANKS):
+            score(b)
+            exponentiate(b)
+        neg_m1 = neg_max[:, BANKS - 1, 0:1]
         fix = sb.tile([P, BANKS], F32, name="fix")
-        nc.scalar.activation(out=fix[:], in_=neg_max[:], func=ACT.Exp, scale=-1.0, bias=neg_m1)
+        nc.scalar.activation(out=fix[:], in_=neg_max[:, :, 0], func=ACT.Exp, scale=-1.0, bias=neg_m1)
 
         picked = sb.tile([P, I], F32, name="picked")
         nc.vector.tensor_copy(out=picked[:], in_=scores[:].indirect(list1[:]))

@@ -176,19 +176,25 @@ def tile_attend_brankshares_heads_kernel(tc, hid, voc_words, voc_scales, sw, old
                 out=placed1[:].indirect(list1[:, entries(h)]), in0=slope[:, slots(h)], in1=px[:, slots(h)], op=ALU.mult
             )
 
-        slope_piece(0)
         weighted_gap = sb.tile([P, I], F32, name="weighted_gap")
-        nc.vector.scalar_tensor_tensor(
-            out=weighted_gap[:], in0=gap[:], scalar=inv_z[:], in1=weight_rate[:], op0=ALU.mult, op1=ALU.mult
-        )
+
+        def weigh_gap(h):
+            nc.vector.scalar_tensor_tensor(
+                out=weighted_gap[:, slots(h)], in0=gap[:, slots(h)], scalar=inv_z[:], in1=weight_rate[:, slots(h)],
+                op0=ALU.mult, op1=ALU.mult,
+            )
+
+        weigh_gap(0)
+        slope_piece(0)
+        weigh_gap(1)
         place1(0)
+        slope_piece(1)
         slope_gap = sb.tile([P, I], F32, name="slope_gap")
         total = sb.tile([P, 1], F32, name="total")
         nc.vector.scalar_tensor_tensor(
             out=slope_gap[:], in0=half_sq[:], scalar=1.0, in1=weighted_gap[:], op0=ALU.subtract, op1=ALU.mult,
             accum_out=total[:],
         )
-        slope_piece(1)
         place1(1)
         nc.vector.tensor_tensor(out=placed2[:].indirect(list2[:]), in0=slope[:], in1=px2[:], op=ALU.mult)
 

from contextlib import ExitStack

import concourse.mybir as mybir
from concourse.masks import make_identity

D, V, Q, I = 512, 2048, 128, 512
FLOPS = 2 * D * Q * V

F32 = mybir.dt.float32
BF16 = mybir.dt.bfloat16
I32 = mybir.dt.int32
U32 = mybir.dt.uint32
U16 = mybir.dt.uint16
U8 = mybir.dt.uint8
FP8X4 = mybir.dt.float8_e4m3fn_x4
FP4X4 = mybir.dt.float4_e2m1fn_x4
ALU = mybir.AluOpType
ACT = mybir.ActivationFunctionType
AXIS = mybir.AxisListType

P = 128
PACK = 4
BANK = 512
BANKS = V // BANK
BLOCKS = BANK // P
LOAD_EDGES = (0, BANK, 2 * BANK, V)
PIECE_EDGES = (0, 128, I)
PIECES = len(PIECE_EDGES) - 1
PER_COLUMN = 16
SPACED = 8


def tile_attend_brankshares_heads_kernel(tc, hid, voc_words, voc_scales, sw, old, offs, offs2, out):
    nc = tc.nc
    with ExitStack() as ctx:
        sb = ctx.enter_context(tc.tile_pool(name="sb", bufs=1))
        ps = ctx.enter_context(tc.psum_pool(name="ps", bufs=1))

        hid_raw = sb.tile([P, PACK, Q], F32, name="hid_raw")
        nc.sync.dma_start(out=hid_raw[:], in_=hid.rearrange("(p t) q -> p t q", t=PACK))

        voc_plane = sb.tile([P, V], U8, name="voc_plane", align_bytes=64)
        nc.gpsimd.memset(voc_plane[:].bitcast(I32), 0)
        for quad in range(4):
            nc.sync.dma_start(
                out=voc_plane[32 * quad : 32 * quad + 4, :].bitcast(I32),
                in_=voc_scales[0, 4 * quad : 4 * quad + 4, :].bitcast(I32),
            )
        words = []
        for first, last in zip(LOAD_EDGES, LOAD_EDGES[1:]):
            part = sb.tile([P, 2 * (last - first)], U8, name="words%d" % first, align_bytes=64)
            nc.sync.dma_start(out=part[:].bitcast(I32), in_=voc_words[0, :, 2 * first : 2 * last].bitcast(I32))
            for start in range(0, last - first, BANK):
                words.append(part[:, 2 * start : 2 * (start + BANK)])
        list1 = sb.tile([P, I // PER_COLUMN], U16, name="list1")
        nc.sync.dma_start(list1[:], offs)
        list2 = sb.tile([P, I // PER_COLUMN], U16, name="list2")
        nc.sync.dma_start(list2[:], offs2)
        weight = sb.tile([P, I], F32, name="weight")
        nc.sync.dma_start(out=weight[:], in_=sw[0].partition_broadcast(P))
        old_sb = sb.tile([P, V], F32, name="old_sb")
        nc.sync.dma_start(out=old_sb[:], in_=old)

        ident = sb.tile([P, P], F32, name="ident")
        make_identity(nc, ident[:])
        placed1 = sb.tile([P, V], F32, name="placed1")
        nc.vector.memset(placed1[:], 0.0)

        hid_bf = sb.tile([P, Q, PACK], BF16, name="hid_bf", tag="hid_then_placed", align_bytes=64)
        hid_codes = sb.tile([P, Q], U32, name="hid_codes", align_bytes=64)
        hid_plane = sb.tile([P, Q], U8, name="hid_plane", align_bytes=64)
        nc.vector.tensor_copy(
            out=hid_bf[:, : Q // 2, :], in_=hid_raw[:, :, : Q // 2].rearrange("p t q -> p q t")
        )
        nc.scalar.copy(out=hid_bf[:, Q // 2 :, :], in_=hid_raw[:, :, Q // 2 :].rearrange("p t q -> p q t"))
        nc.vector.quantize_mx(
            out=hid_codes[:].bitcast(FP8X4), scales=hid_plane[:], in_=hid_bf[:].rearrange("p q t -> p (q t)")
        )
        placed2 = sb.tile([P, V], F32, name="placed2", tag="hid_then_placed", align_bytes=64)
        nc.vector.memset(placed2[:], 0.0)

        scores = sb.tile([P, V], F32, name="scores")
        bank_max = sb.tile([P, BANKS], F32, name="bank_max")
        shares = sb.tile([P, V], F32, name="shares")

        def columns(b):
            return slice(b * BANK, (b + 1) * BANK)

        def score(b):
            acc = ps.tile([P, BANK], F32, name="upright%d" % b, tag="upright%d" % b)
            nc.tensor.matmul_mx(
                out=acc[:],
                lhsT=hid_codes[:].bitcast(FP8X4),
                lhsT_scale=hid_plane[:],
                rhs=words[b].bitcast(FP4X4),
                rhs_scale=voc_plane[:, columns(b)],
                start=True,
                stop=True,
            )
            nc.vector.tensor_scalar(
                out=scores[:, columns(b)], in0=acc[:], scalar1=1.0, scalar2=None,
                op0=ALU.mult, op1=ALU.max, accum_out=bank_max[:, b : b + 1],
            )

        neg_max = sb.tile([P, BANKS, SPACED], F32, name="neg_max")
        bank_sum = sb.tile([P, BANKS], F32, name="bank_sum")

        def exponentiate(b):
            if b < BANKS - 1:
                nc.gpsimd.tensor_scalar(
                    out=neg_max[:, b, 0:1], in0=bank_max[:, b : b + 1], scalar1=-1.0, scalar2=0.0,
                    op0=ALU.mult, op1=ALU.add,
                )
            else:
                nc.vector.tensor_reduce(
                    out=neg_max[:, b, 0:1], in_=bank_max[:], axis=AXIS.X, op=ALU.max, negate=True
                )
            nc.scalar.activation(
                out=shares[:, columns(b)], in_=scores[:, columns(b)], func=ACT.Exp,
                bias=neg_max[:, b, 0:1], accum_out=bank_sum[:, b : b + 1],
            )

        for b in range(BANKS):
            score(b)
            exponentiate(b)
        neg_m1 = neg_max[:, BANKS - 1, 0:1]
        fix = sb.tile([P, BANKS], F32, name="fix")
        nc.scalar.activation(out=fix[:], in_=neg_max[:, :, 0], func=ACT.Exp, scale=-1.0, bias=neg_m1)

        picked = sb.tile([P, I], F32, name="picked")
        nc.vector.tensor_copy(out=picked[:], in_=scores[:].indirect(list1[:]))
        px2 = sb.tile([P, I], F32, name="px2")
        nc.scalar.activation(out=px2[:], in_=scores[:].indirect(list2[:]), func=ACT.Exp, bias=neg_m1)

        terms = sb.tile([P, BANKS], F32, name="terms")
        z = sb.tile([P, 1], F32, name="z")
        nc.vector.scalar_tensor_tensor(
            out=terms[:], in0=fix[:], scalar=1.0, in1=bank_sum[:], op0=ALU.mult, op1=ALU.mult, accum_out=z[:]
        )
        inv_z = sb.tile([P, 1], F32, name="inv_z")
        nc.vector.reciprocal(out=inv_z[:], in_=z[:])
        rate = sb.tile([P, 1], F32, name="rate")
        nc.vector.tensor_scalar(out=rate[:], in0=inv_z[:], scalar1=256.0, scalar2=None, op0=ALU.mult)
        weight_rate = sb.tile([P, I], F32, name="weight_rate")
        nc.vector.tensor_scalar(
            out=weight_rate[:], in0=weight[:], scalar1=inv_z[:], scalar2=256.0, op0=ALU.mult, op1=ALU.mult
        )

        px = sb.tile([P, I], F32, name="px")
        gap = sb.tile([P, I], F32, name="gap")
        half = sb.tile([P, I], F32, name="half")
        half_sq = sb.tile([P, I], F32, name="half_sq")
        slope = sb.tile([P, I], F32, name="slope")

        def slots(h):
            return slice(PIECE_EDGES[h], PIECE_EDGES[h + 1])

        def entries(h):
            return slice(PIECE_EDGES[h] // PER_COLUMN, PIECE_EDGES[h + 1] // PER_COLUMN)

        for h in range(PIECES):
            nc.scalar.activation(out=px[:, slots(h)], in_=picked[:, slots(h)], func=ACT.Exp, bias=neg_m1)
        for h in range(PIECES):
            nc.vector.tensor_tensor(out=gap[:, slots(h)], in0=px2[:, slots(h)], in1=px[:, slots(h)], op=ALU.subtract)
            nc.scalar.activation(out=half[:, slots(h)], in_=gap[:, slots(h)], func=ACT.Tanh, scale=rate[:])
            nc.scalar.activation(out=half_sq[:, slots(h)], in_=half[:, slots(h)], func=ACT.Square)

        def slope_piece(h):
            nc.vector.scalar_tensor_tensor(
                out=slope[:, slots(h)], in0=half_sq[:, slots(h)], scalar=1.0, in1=weight_rate[:, slots(h)],
                op0=ALU.subtract, op1=ALU.mult,
            )

        def place1(h):
            nc.vector.tensor_tensor(
                out=placed1[:].indirect(list1[:, entries(h)]), in0=slope[:, slots(h)], in1=px[:, slots(h)], op=ALU.mult
            )

        weighted_gap = sb.tile([P, I], F32, name="weighted_gap")

        def weigh_gap(h):
            nc.vector.scalar_tensor_tensor(
                out=weighted_gap[:, slots(h)], in0=gap[:, slots(h)], scalar=inv_z[:], in1=weight_rate[:, slots(h)],
                op0=ALU.mult, op1=ALU.mult,
            )

        weigh_gap(0)
        slope_piece(0)
        weigh_gap(1)
        place1(0)
        slope_piece(1)
        slope_gap = sb.tile([P, I], F32, name="slope_gap")
        total = sb.tile([P, 1], F32, name="total")
        nc.vector.scalar_tensor_tensor(
            out=slope_gap[:], in0=half_sq[:], scalar=1.0, in1=weighted_gap[:], op0=ALU.subtract, op1=ALU.mult,
            accum_out=total[:],
        )
        place1(1)
        nc.vector.tensor_tensor(out=placed2[:].indirect(list2[:]), in0=slope[:], in1=px2[:], op=ALU.mult)

        factor = sb.tile([P, BANKS - 1], F32, name="factor")
        nc.scalar.activation(out=factor[:], in_=fix[:, 0 : BANKS - 1], func=ACT.Copy, scale=total[:])
        spread = sb.tile([P, V], F32, name="spread")
        order = [BANKS - 1] + list(range(BANKS - 1))
        for b in order:
            nc.scalar.activation(
                out=spread[:, columns(b)], in_=shares[:, columns(b)], func=ACT.Copy,
                scale=total[:] if b == BANKS - 1 else factor[:, b : b + 1],
            )

        turned = [ps.tile([P, BANK], F32, name="turned%d" % b, tag="turned%d" % b) for b in range(BANKS)]
        addends = [old_sb, spread, placed1]

        def add_turned(b, n):
            for j in range(BLOCKS):
                first = b * BANK + j * P
                nc.tensor.matmul(
                    turned[b][:, j * P : (j + 1) * P], addends[n][:, first : first + P], ident[:],
                    start=(n == 0 and j == 0), stop=(n == len(addends) - 1 and j == BLOCKS - 1),
                    is_transpose=True,
                )

        for n in range(len(addends) - 1):
            for b in order:
                add_turned(b, n)

        turned_sb = sb.tile([P, V], F32, name="turned_sb")
        result = sb.tile([P, V], F32, name="result")

        def close_sum(b):
            add_turned(b, len(addends) - 1)
            nc.scalar.copy(out=turned_sb[:, columns(b)], in_=turned[b][:])

        def finish(b):
            back = ps.tile([P, BANK], F32, name="back%d" % b, tag="upright%d" % b)
            for j in range(BLOCKS):
                first = b * BANK + j * P
                nc.tensor.transpose(back[:, j * P : (j + 1) * P], turned_sb[:, first : first + P], ident[:])
            nc.vector.tensor_tensor(
                out=result[:, columns(b)], in0=back[:], in1=placed2[:, columns(b)], op=ALU.subtract
            )
            nc.sync.dma_start(out=out[:, columns(b)], in_=result[:, columns(b)])

        for b in range(BANKS + 2):
            if b < BANKS:
                close_sum(order[b])
            if b > 1:
                finish(order[b - 2])
